import numpy as np
import ml_dtypes


def mxq(x, axis, fmt="e4m3"):
    dtype, down = {"e4m3": (ml_dtypes.float8_e4m3fn, 7), "e5m2": (ml_dtypes.float8_e5m2, 14)}[fmt]
    v = np.moveaxis(np.asarray(x, np.float32).astype(ml_dtypes.bfloat16).astype(np.float64), axis, -1)
    blocks = v.reshape(v.shape[:-1] + (-1, 32))
    amax = np.abs(blocks).max(-1, keepdims=True)
    byte = np.maximum(np.where(amax > 0, np.frexp(amax)[1] - 1 + 127, 0) - down, 1)
    scale = np.exp2(byte - 127.0)
    codes = (blocks / scale).astype(np.float32).astype(dtype).astype(np.float64)
    return np.moveaxis((codes * scale).reshape(v.shape), -1, axis)


WIDE = False


def mx_kscale(k):
    if not WIDE:
        return np.ones(k)
    levels = np.array([10, -10, 5, -5, 0])
    if k % 512:
        return np.exp2(np.random.permutation(np.resize(levels, k // 32))).repeat(32)
    a = np.empty((k // 512, 16))
    for p in range(k // 512):
        a[p, :8] = np.random.permutation(np.resize(levels, 8))
        for g in range(8):
            far = levels[np.abs(levels - a[p, g]) >= 10]
            a[p, g + 8] = far[np.random.randint(len(far))]
    return np.exp2(a.ravel()).repeat(32)


def f64(x):
    return np.asarray(x).astype(np.float64)


def striped(idx):
    return np.tile(idx.reshape(-1, 16).T, (8, 1)).astype(np.uint16)


def unstriped(offs):
    return offs[:16].T.reshape(-1).astype(np.int64)


def striped8(idx):
    return np.concatenate([x.reshape(-1, 16).T for x in idx]).astype(np.uint16)


def runs(offs, k):
    lists = np.stack([offs[16 * r : 16 * r + 16].T.reshape(-1) for r in range(8)]).astype(np.int64)
    return lists[np.arange(k) % 512 // 64]


def pack_weight(w):
    k, n = w.shape
    w = f64(np.asarray(w, np.float32).astype(ml_dtypes.bfloat16)).reshape(k // 32, 32, n)
    amax = np.abs(w).max(1)
    byte = np.clip(np.where(amax > 0, np.frexp(amax)[1] - 1 + 127 - 7, 1), 1, 254)
    scaled = (w * np.exp2(127.0 - byte)[:, None, :]).reshape(k, n).astype(np.float32)
    words = np.ascontiguousarray(scaled.reshape(k // 512, 128, 4, n).transpose(0, 1, 3, 2)).astype(ml_dtypes.float8_e4m3fn).view(np.uint8)
    return words, np.ascontiguousarray(byte.astype(np.uint8).reshape(k // 512, 16, n))


def unpack_weight(words, scales):
    g, p, n, _ = words.shape
    vals = np.ascontiguousarray(words).view(ml_dtypes.float8_e4m3fn).astype(np.float64) * np.repeat(np.exp2(scales.astype(np.float64) - 127.0), 8, axis=1)[..., None]
    return vals.transpose(0, 1, 3, 2).reshape(g * 512, n)


K, T, S, N, H, W = 512, 2048, 512, 512, 512, 256


def setup_inputs():
    n = np.random.standard_normal
    s = mx_kscale(K)[:, None]
    u = mx_kscale(H)
    packed_xT = pack_weight(n((K, T)) * s)
    return {
        "x_words": packed_xT[0],
        "x_scales": packed_xT[1],
        "w1": (n((K, H)) / np.sqrt(K) / s).astype(np.float32),
        "gn": (np.random.uniform(0.5, 1.5, (H, 1)) * u[:, None]).astype(np.float32),
        "w2": (n((H, N)) / np.sqrt(H) / u[:, None]).astype(np.float32),
        "offs": striped(np.random.permutation(T)[:S]),
        "n1": striped8(np.stack([np.random.permutation(S) for _ in range(8)])),
        "n2": striped8(np.stack([np.random.permutation(S) for _ in range(8)])),
        "n3": striped8(np.stack([np.random.permutation(S)[:W] for _ in range(8)])),
        "n4": striped8(np.stack([np.random.permutation(S)[:W] for _ in range(8)])),
    }


def reference(x_words, x_scales, w1, gn, w2, offs, n1, n2, n3, n4):
    xq = unpack_weight(x_words, x_scales)[:, unstriped(offs)]
    y = mxq(f64(w1), 0, "e4m3").T @ xq
    pa = y[np.arange(H)[:, None], runs(n1, H)]
    kr = np.exp(-0.5 * ((y - pa) ** 2))
    pb = y[np.arange(H)[:, None], runs(n2, H)]
    kr2 = np.exp(-0.5 * ((y - pb) ** 2))
    z = f64(gn) * ((kr * pa + kr2 * pb) / (kr + kr2 + 0.5))
    h = mxq(f64(w2), 0, "e4m3").T @ mxq(z, 0, "e4m3")
    ra = y[np.arange(H)[:, None], runs(n4, H)] - (0.5 * (h[np.arange(N)[:, None], runs(n3, N)]))
    out = h.copy()
    out[np.arange(H)[:, None], runs(n3, H)] = ra
    return out

@@ -1,0 +1,176 @@
+from contextlib import ExitStack
+
+import concourse.mybir as mybir
+from concourse.masks import make_identity
+
+F32 = mybir.dt.float32
+BF16 = mybir.dt.bfloat16
+I32 = mybir.dt.int32
+U32 = mybir.dt.uint32
+U16 = mybir.dt.uint16
+U8 = mybir.dt.uint8
+FP8X4 = mybir.dt.float8_e4m3fn_x4
+ALU = mybir.AluOpType
+ACT = mybir.ActivationFunctionType
+
+P = 128
+PACK = 4
+K, T, S, N, H, W = 512, 2048, 512, 512, 512, 256
+FLOPS = 2 * K * H * S + 2 * H * N * S
+HALF = S // 2
+
+
+def tile_picked_skipputbkern_none_p_kernel(tc, x_words, x_scales, w1, gn, w2, offs, n1, n2, n3, n4, out):
+    nc = tc.nc
+    with ExitStack() as ctx:
+        keep = ctx.enter_context(tc.tile_pool(name="keep", bufs=1))
+        work = ctx.enter_context(tc.tile_pool(name="work", bufs=2))
+        psum = ctx.enter_context(tc.psum_pool(name="psum", bufs=1))
+
+        offs_t = keep.tile([P, S // 16], U16, name="offs_t")
+        n1_t = keep.tile([P, S // 16], U16, name="n1_t")
+        n2_t = keep.tile([P, S // 16], U16, name="n2_t")
+        n3_t = keep.tile([P, W // 16], U16, name="n3_t")
+        n4_t = keep.tile([P, W // 16], U16, name="n4_t")
+        gn_t = keep.tile([P, PACK], F32, name="gn_t")
+        xw = keep.tile([P, T], I32, name="xw", align_bytes=64)
+        xs = keep.tile([P, T], U8, name="xs", align_bytes=64)
+        w1_raw = [keep.tile([P, PACK, H // 2], F32, name=f"w1_raw{h}") for h in range(2)]
+        w2_raw = keep.tile([P, PACK, N], F32, name="w2_raw")
+        y = [keep.tile([P, 2 * S], F32, name=f"y{t}") for t in range(PACK)]
+
+        nc.vector.memset(xs[:].bitcast(I32), 0)
+        w1v = w1.rearrange("(p j) c -> p j c", j=PACK)
+        nc.sync.dma_start(out=w1_raw[0][:], in_=w1v[:, :, : H // 2])
+        for q in range(4):
+            nc.sync.dma_start(out=xs[32 * q : 32 * q + 4, :].bitcast(I32), in_=x_scales[0, 4 * q : 4 * q + 4, :].bitcast(I32))
+        nc.sync.dma_start(out=offs_t[:], in_=offs)
+        nc.sync.dma_start(out=w1_raw[1][:], in_=w1v[:, :, H // 2 :])
+        nc.sync.dma_start(out=xw[:], in_=x_words[0].rearrange("p n t -> p (n t)").bitcast(I32))
+        nc.sync.dma_start(out=n1_t[:], in_=n1)
+        nc.sync.dma_start(out=n2_t[:], in_=n2)
+        nc.sync.dma_start(out=gn_t[:], in_=gn.rearrange("(p t) o -> p (t o)", t=PACK))
+        nc.sync.dma_start(out=w2_raw[:], in_=w2.rearrange("(p j) c -> p j c", j=PACK))
+        nc.sync.dma_start(out=n4_t[:], in_=n4)
+        nc.sync.dma_start(out=n3_t[:], in_=n3)
+        for t in range(PACK):
+            nc.gpsimd.memset(y[t][:, S:], 0.0)
+        ident = keep.tile([P, P], F32, name="ident")
+        make_identity(nc, ident[:])
+
+        w1_bf = keep.tile([P, PACK, P, PACK], BF16, name="w1_bf", align_bytes=64)
+        w1_walk = w1_bf[:].rearrange("p t m j -> p m j t")
+        nc.scalar.copy(out=w1_walk[:, : P // 2], in_=w1_raw[0][:].rearrange("p j (m t) -> p m j t", t=PACK))
+        nc.vector.tensor_copy(out=w1_walk[:, P // 2 :], in_=w1_raw[1][:].rearrange("p j (m t) -> p m j t", t=PACK))
+        w1_codes = keep.tile([P, H], U32, name="w1_codes", align_bytes=64)
+        w1_scales = keep.tile([P, H], U8, name="w1_scales", align_bytes=64)
+        xg_scales = keep.tile([P, S], U8, name="xg_scales", align_bytes=64)
+        nc.vector.tensor_copy(out=xg_scales[:], in_=xs[:].indirect(offs_t[:]))
+        nc.vector.quantize_mx(out=w1_codes[:].bitcast(FP8X4), scales=w1_scales[:], in_=w1_bf[:].rearrange("p t m j -> p (t m j)"))
+
+        y_ps = [psum.tile([P, S], F32, name=f"y_ps{t}", tag=f"bank{t}") for t in range(PACK)]
+        for h in range(2):
+            xg = keep.tile([P, HALF], U32, name=f"xg{h}", tag=f"xg{h}", align_bytes=64)
+            nc.vector.tensor_copy(out=xg[:], in_=xw[:].bitcast(U32).indirect(offs_t[:, h * (HALF // 16) : (h + 1) * (HALF // 16)]))
+            cols = slice(h * HALF, (h + 1) * HALF)
+            for t in range(PACK):
+                m = slice(t * P, (t + 1) * P)
+                nc.tensor.matmul_mx(out=y_ps[t][:, cols], lhsT=w1_codes[:, m].bitcast(FP8X4), lhsT_scale=w1_scales[:, m],
+                                    rhs=xg[:].bitcast(FP8X4), rhs_scale=xg_scales[:, cols], start=True, stop=True)
+        for t in range(PACK):
+            nc.scalar.copy(out=y[t][:, :S], in_=y_ps[t][:])
+
+        w2_bf = keep.tile([P, PACK, P, PACK], BF16, name="w2_bf", tag="xg1", align_bytes=64)
+        w2_walk = w2_bf[:].rearrange("p t m j -> p m j t")
+        w2_src = w2_raw[:].rearrange("p j (m t) -> p m j t", t=PACK)
+        w2_codes = keep.tile([P, N], U32, name="w2_codes", align_bytes=64)
+        w2_scales = keep.tile([P, N], U8, name="w2_scales", align_bytes=64)
+        pab = [keep.tile([P, 2, S], F32, name=f"pab{t}") for t in range(PACK)]
+        kr = [keep.tile([P, 2, S], F32, name=f"kr{t}") for t in range(PACK)]
+
+        def add_turned(banks, src, e):
+            for g in range(2):
+                for c in range(2):
+                    cols = slice((2 * g + c) * P, (2 * g + c + 1) * P)
+                    for a in range(2):
+                        nc.tensor.matmul(banks[g][:, c, e, :], lhsT=src[:, a, cols], rhs=ident[:], start=(a == 0), stop=(a == 1), is_transpose=True)
+
+        den2 = {}
+        for u in range(2):
+            ksum = [psum.tile([P, 2, 2, P], F32, name=f"ksum{u}{g}", tag=f"bank{4 + g}") for g in range(2)]
+            for e in range(2):
+                t = 2 * u + e
+                nc.vector.tensor_copy(out=pab[t][:, 0, :], in_=y[t][:].indirect(n1_t[:]))
+                nc.vector.tensor_copy(out=pab[t][:, 1, :], in_=y[t][:].indirect(n2_t[:]))
+                d = work.tile([P, 2, S], F32, name="d", tag="d")
+                nc.vector.tensor_tensor(out=d[:], in0=pab[t][:], in1=y_ps[t][:].unsqueeze(1).to_broadcast([P, 2, S]), op=ALU.subtract)
+                dsq = keep.tile([P, 2, S], F32, name="dsq", tag="dsq")
+                nc.scalar.activation(out=dsq[:], in_=d[:], func=ACT.Square)
+                nc.scalar.activation(out=kr[t][:], in_=dsq[:], func=ACT.Exp, scale=-0.5)
+                add_turned(ksum, kr[t], e)
+                if t < 2:
+                    ms = slice(t * (P // 2), (t + 1) * (P // 2))
+                    nc.scalar.copy(out=w2_walk[:, ms], in_=w2_src[:, ms])
+            for g in range(2):
+                den2[u, g] = keep.tile([P, 2, P, 2], F32, name=f"den2_{u}{g}")
+                nc.scalar.activation(out=den2[u, g][:], in_=ksum[g][:].rearrange("p c e m -> p c m e"), func=ACT.Square, bias=0.5)
+
+        num = {}
+        for u in range(2):
+            banks = [psum.tile([P, 2, 2, P], F32, name=f"num{u}{g}", tag=f"bank{2 * u + g}") for g in range(2)]
+            for e in range(2):
+                t = 2 * u + e
+                prod = work.tile([P, 2, S], F32, name="prod", tag="d")
+                nc.vector.scalar_tensor_tensor(out=prod[:], in0=kr[t][:], scalar=gn_t[:, t : t + 1], in1=pab[t][:], op0=ALU.mult, op1=ALU.mult)
+                add_turned(banks, prod, e)
+            for g in range(2):
+                num[u, g] = banks[g]
+        nc.vector.quantize_mx(out=w2_codes[:].bitcast(FP8X4), scales=w2_scales[:], in_=w2_bf[:].rearrange("p t m j -> p (t m j)"))
+
+        rec_all = keep.tile([P, 4, 2, P, 2], F32, name="rec_all", tag="dsq")
+        rec = {}
+        for g in range(2):
+            for u in range(2):
+                rec[u, g] = rec_all[:, 2 * g + u]
+                nc.scalar.activation(out=rec[u, g], in_=den2[u, g][:], func=ACT.Abs_reciprocal_sqrt)
+
+        z_codes, z_scales = [], []
+        for g in range(2):
+            z_ps = psum.tile([P, 2, 2, P], F32, name=f"z_ps{g}", tag=f"bank{6 + g}")
+            for u in range(2):
+                zt = keep.tile([P, 2, P, 2], BF16, name=f"zt{u}{g}")
+                nc.vector.tensor_tensor(out=zt[:], in0=num[u, g][:].rearrange("p c e m -> p c m e"), in1=rec[u, g], op=ALU.mult)
+                words = zt[:].rearrange("p c m e -> p (c m e)").bitcast(F32)
+                for c in range(2):
+                    nc.tensor.transpose(z_ps[:, u, c, :], words[:, c * P : (c + 1) * P], ident[:])
+            z_bf = keep.tile([P, HALF * PACK], BF16, name=f"z_bf{g}", tag=f"z_bf{g}", align_bytes=64)
+            nc.scalar.copy(out=z_bf[:].bitcast(F32).rearrange("p (n u) -> p n u", u=2), in_=z_ps[:].rearrange("p u c n -> p (c n) u"))
+            z_codes.append(keep.tile([P, HALF], U32, name=f"z_codes{g}", align_bytes=64))
+            z_scales.append(keep.tile([P, HALF], U8, name=f"z_scales{g}", align_bytes=64))
+            nc.vector.quantize_mx(out=z_codes[g][:].bitcast(FP8X4), scales=z_scales[g][:], in_=z_bf[:])
+
+        h_ps = [psum.tile([P, S], F32, name=f"h_ps{t}", tag=f"bank{(4, 5, 0, 2)[t]}") for t in range(PACK)]
+        for g in range(2):
+            cols = slice(g * HALF, (g + 1) * HALF)
+            for t in range(PACK):
+                m = slice(t * P, (t + 1) * P)
+                nc.tensor.matmul_mx(out=h_ps[t][:, cols], lhsT=w2_codes[:, m].bitcast(FP8X4), lhsT_scale=w2_scales[:, m],
+                                    rhs=z_codes[g][:].bitcast(FP8X4), rhs_scale=z_scales[g][:], start=True, stop=True)
+
+        y4a = keep.tile([P, W], F32, name="y4a", tag="dsq")
+        y4b = keep.tile([P, W], F32, name="y4b", tag="z_bf0", align_bytes=64)
+        y4c = keep.tile([P, 2, W], F32, name="y4c", tag="z_bf1", align_bytes=64)
+        y4 = [y4a[:], y4b[:], y4c[:, 0, :], y4c[:, 1, :]]
+        for t in range(PACK):
+            nc.vector.tensor_copy(out=y4[t], in_=y[t][:].indirect(n4_t[:]))
+
+        outv = out.rearrange("(p t) n -> p t n", t=PACK)
+        hs = [keep.tile([P, S], F32, name=f"hs{t}") for t in range(PACK)]
+        h3 = [keep.tile([P, W], F32, name=f"h3_{t}") for t in range(PACK)]
+        for t in range(PACK):
+            nc.scalar.copy(out=hs[t][:], in_=h_ps[t][:])
+        for t in range(PACK):
+            nc.vector.tensor_scalar(out=h3[t][:], in0=hs[t][:].indirect(n3_t[:]), scalar1=-0.5, scalar2=0.0, op0=ALU.mult, op1=ALU.add)
+        for t in range(PACK):
+            nc.vector.tensor_tensor(out=hs[t][:].indirect(n3_t[:]), in0=h3[t][:], in1=y4[t], op=ALU.add)
+            nc.sync.dma_start(out=outv[:, t, :], in_=hs[t][:])

@@ -15,9 +15,14 @@ ACT = mybir.ActivationFunctionType
 
 P = 128
 PACK = 4
+LAST = PACK - 1
+QUADRANTS = 4
+SCALE_ROWS = 4
+STRIPE = 16
+MX_ALIGN = 64
 K, T, S, N, H, W = 512, 2048, 512, 512, 512, 256
-FLOPS = 2 * K * H * S + 2 * H * N * S
 HALF = S // 2
+FLOPS = 2 * K * H * S + 2 * H * N * S
 
 
 def tile_picked_skipputbkern_none_p_kernel(tc, x_words, x_scales, w1, gn, w2, offs, n1, n2, n3, n4, out):
@@ -27,25 +32,26 @@ def tile_picked_skipputbkern_none_p_kernel(tc, x_words, x_scales, w1, gn, w2, of
         work = ctx.enter_context(tc.tile_pool(name="work", bufs=2))
         psum = ctx.enter_context(tc.psum_pool(name="psum", bufs=1))
 
-        offs_t = keep.tile([P, S // 16], U16, name="offs_t")
-        n1_t = keep.tile([P, S // 16], U16, name="n1_t")
-        n2_t = keep.tile([P, S // 16], U16, name="n2_t")
-        n3_t = keep.tile([P, W // 16], U16, name="n3_t")
-        n4_t = keep.tile([P, W // 16], U16, name="n4_t")
+        offs_t = keep.tile([P, S // STRIPE], U16, name="offs_t")
+        n1_t = keep.tile([P, S // STRIPE], U16, name="n1_t")
+        n2_t = keep.tile([P, S // STRIPE], U16, name="n2_t")
+        n3_t = keep.tile([P, W // STRIPE], U16, name="n3_t")
+        n4_t = keep.tile([P, W // STRIPE], U16, name="n4_t")
         gn_t = keep.tile([P, PACK], F32, name="gn_t")
-        xw = keep.tile([P, T], I32, name="xw", align_bytes=64)
-        xs = keep.tile([P, T], U8, name="xs", align_bytes=64)
+        xw = keep.tile([P, T], I32, name="xw", align_bytes=MX_ALIGN)
+        xs = keep.tile([P, T], U8, name="xs", align_bytes=MX_ALIGN)
         w1_raw = [keep.tile([P, PACK, H // 2], F32, name=f"w1_raw{h}") for h in range(2)]
         w2_raw = keep.tile([P, PACK, N], F32, name="w2_raw")
-        y = [keep.tile([P, 2 * S], F32, name=f"y{t}") for t in range(PACK)]
+        y = [keep.tile([P, 2 * S], F32, name=f"y{t}", tag=f"y{t}") for t in range(PACK)]
 
-        nc.vector.memset(xs[:].bitcast(I32), 0)
-        w1v = w1.rearrange("(p j) c -> p j c", j=PACK)
-        nc.sync.dma_start(out=w1_raw[0][:], in_=w1v[:, :, : H // 2])
-        for q in range(4):
-            nc.sync.dma_start(out=xs[32 * q : 32 * q + 4, :].bitcast(I32), in_=x_scales[0, 4 * q : 4 * q + 4, :].bitcast(I32))
+        nc.gpsimd.memset(xs[:].bitcast(I32), 0)
+        w1_rows = w1.rearrange("(p j) c -> p j c", j=PACK)
+        nc.sync.dma_start(out=w1_raw[0][:], in_=w1_rows[:, :, : H // 2])
+        nc.sync.dma_start(out=w1_raw[1][:], in_=w1_rows[:, :, H // 2 :])
+        for q in range(QUADRANTS):
+            rows = x_scales[0, SCALE_ROWS * q : SCALE_ROWS * (q + 1), :]
+            nc.sync.dma_start(out=xs[32 * q : 32 * q + SCALE_ROWS, :].bitcast(I32), in_=rows.bitcast(I32))
         nc.sync.dma_start(out=offs_t[:], in_=offs)
-        nc.sync.dma_start(out=w1_raw[1][:], in_=w1v[:, :, H // 2 :])
         nc.sync.dma_start(out=xw[:], in_=x_words[0].rearrange("p n t -> p (n t)").bitcast(I32))
         nc.sync.dma_start(out=n1_t[:], in_=n1)
         nc.sync.dma_start(out=n2_t[:], in_=n2)
@@ -58,119 +64,187 @@ def tile_picked_skipputbkern_none_p_kernel(tc, x_words, x_scales, w1, gn, w2, of
         ident = keep.tile([P, P], F32, name="ident")
         make_identity(nc, ident[:])
 
-        w1_bf = keep.tile([P, PACK, P, PACK], BF16, name="w1_bf", align_bytes=64)
+        w1_bf = keep.tile([P, PACK, P, PACK], BF16, name="w1_bf", align_bytes=MX_ALIGN)
         w1_walk = w1_bf[:].rearrange("p t m j -> p m j t")
         nc.scalar.copy(out=w1_walk[:, : P // 2], in_=w1_raw[0][:].rearrange("p j (m t) -> p m j t", t=PACK))
         nc.vector.tensor_copy(out=w1_walk[:, P // 2 :], in_=w1_raw[1][:].rearrange("p j (m t) -> p m j t", t=PACK))
-        w1_codes = keep.tile([P, H], U32, name="w1_codes", align_bytes=64)
-        w1_scales = keep.tile([P, H], U8, name="w1_scales", align_bytes=64)
-        xg_scales = keep.tile([P, S], U8, name="xg_scales", align_bytes=64)
+        w1_codes = keep.tile([P, H], U32, name="w1_codes", align_bytes=MX_ALIGN)
+        w1_scales = keep.tile([P, H], U8, name="w1_scales", align_bytes=MX_ALIGN)
+        xg_scales = keep.tile([P, S], U8, name="xg_scales", align_bytes=MX_ALIGN)
         nc.vector.tensor_copy(out=xg_scales[:], in_=xs[:].indirect(offs_t[:]))
         nc.vector.quantize_mx(out=w1_codes[:].bitcast(FP8X4), scales=w1_scales[:], in_=w1_bf[:].rearrange("p t m j -> p (t m j)"))
 
-        y_ps = [psum.tile([P, S], F32, name=f"y_ps{t}", tag=f"bank{t}") for t in range(PACK)]
+        xg = [keep.tile([P, HALF], U32, name=f"xg{h}", tag=f"xg{h}", align_bytes=MX_ALIGN) for h in range(2)]
         for h in range(2):
-            xg = keep.tile([P, HALF], U32, name=f"xg{h}", tag=f"xg{h}", align_bytes=64)
-            nc.vector.tensor_copy(out=xg[:], in_=xw[:].bitcast(U32).indirect(offs_t[:, h * (HALF // 16) : (h + 1) * (HALF // 16)]))
+            entries = offs_t[:, h * (HALF // STRIPE) : (h + 1) * (HALF // STRIPE)]
+            nc.vector.tensor_copy(out=xg[h][:], in_=xw[:].bitcast(U32).indirect(entries))
+        y_ps = {}
+        y_ps_last = psum.tile([P, S], F32, name="y_ps_last", tag=f"bank{LAST}")
+        passes = [(0, 0)] + [step for t in range(1, LAST) for step in ((t, 0), (t - 1, 1))] + [(LAST - 1, 1), (LAST, 0), (LAST, 1)]
+        for t, h in passes:
             cols = slice(h * HALF, (h + 1) * HALF)
-            for t in range(PACK):
-                m = slice(t * P, (t + 1) * P)
-                nc.tensor.matmul_mx(out=y_ps[t][:, cols], lhsT=w1_codes[:, m].bitcast(FP8X4), lhsT_scale=w1_scales[:, m],
-                                    rhs=xg[:].bitcast(FP8X4), rhs_scale=xg_scales[:, cols], start=True, stop=True)
-        for t in range(PACK):
-            nc.scalar.copy(out=y[t][:, :S], in_=y_ps[t][:])
+            features = slice(t * P, (t + 1) * P)
+            if t < LAST:
+                y_ps[t, h] = psum.tile([P, HALF], F32, name=f"y_ps{h}{t}", tag=f"bank{PACK * h + t}")[:]
+            else:
+                y_ps[t, h] = y_ps_last[:, cols]
+            nc.tensor.matmul_mx(out=y_ps[t, h], lhsT=w1_codes[:, features].bitcast(FP8X4), lhsT_scale=w1_scales[:, features],
+                                rhs=xg[h][:].bitcast(FP8X4), rhs_scale=xg_scales[:, cols], start=True, stop=True)
+        vector_copy = (1, 0)
+        for t in range(LAST):
+            for h in range(2):
+                cols = slice(h * HALF, (h + 1) * HALF)
+                if (t, h) == vector_copy:
+                    nc.vector.tensor_copy(out=y[t][:, cols], in_=y_ps[t, h])
+                else:
+                    nc.scalar.copy(out=y[t][:, cols], in_=y_ps[t, h])
+        nc.scalar.copy(out=y[LAST][:, :S], in_=y_ps_last[:])
 
-        w2_bf = keep.tile([P, PACK, P, PACK], BF16, name="w2_bf", tag="xg1", align_bytes=64)
-        w2_walk = w2_bf[:].rearrange("p t m j -> p m j t")
         w2_src = w2_raw[:].rearrange("p j (m t) -> p m j t", t=PACK)
-        w2_codes = keep.tile([P, N], U32, name="w2_codes", align_bytes=64)
-        w2_scales = keep.tile([P, N], U8, name="w2_scales", align_bytes=64)
-        pab = [keep.tile([P, 2, S], F32, name=f"pab{t}") for t in range(PACK)]
-        kr = [keep.tile([P, 2, S], F32, name=f"kr{t}") for t in range(PACK)]
+        w2_bf = [keep.tile([P, 2, P, PACK], BF16, name="w2_bf0", tag="xg1", align_bytes=MX_ALIGN)]
+        nc.scalar.copy(out=w2_bf[0][:].rearrange("p e m j -> p m j e"), in_=w2_src[:, :, :, 0:2])
 
-        def add_turned(banks, src, e):
-            for g in range(2):
-                for c in range(2):
-                    cols = slice((2 * g + c) * P, (2 * g + c + 1) * P)
-                    for a in range(2):
-                        nc.tensor.matmul(banks[g][:, c, e, :], lhsT=src[:, a, cols], rhs=ident[:], start=(a == 0), stop=(a == 1), is_transpose=True)
+        w2_scales = keep.tile([P, N], U8, name="w2_scales", align_bytes=MX_ALIGN)
+        pab = [keep.tile([P, 2, S], F32, name=f"pab{t}", tag=f"pab{t}", align_bytes=MX_ALIGN) for t in range(PACK)]
+        kr = [keep.tile([P, 2, S], F32, name=f"kr{t}", tag=f"kr{t}", align_bytes=MX_ALIGN) for t in range(PACK)]
 
-        den2 = {}
+        def add_turned(bank, src, e, g):
+            for c in range(2):
+                places = slice((2 * g + c) * P, (2 * g + c + 1) * P)
+                for a in range(2):
+                    nc.tensor.matmul(bank[:, c, e, :], lhsT=src[:, a, places], rhs=ident[:], start=(a == 0), stop=(a == 1), is_transpose=True)
+
+        ksum, den2 = {}, {}
+
+        def square_den(u, g):
+            den2[u, g] = keep.tile([P, 2, P, 2], F32, name=f"den2_{u}{g}", tag=f"den2_{u}{g}", align_bytes=MX_ALIGN)
+            nc.scalar.activation(out=den2[u, g][:], in_=ksum[u, g][:].rearrange("q c e p -> q c p e"), func=ACT.Square, bias=0.5)
+
         for u in range(2):
-            ksum = [psum.tile([P, 2, 2, P], F32, name=f"ksum{u}{g}", tag=f"bank{4 + g}") for g in range(2)]
-            for e in range(2):
-                t = 2 * u + e
-                nc.vector.tensor_copy(out=pab[t][:, 0, :], in_=y[t][:].indirect(n1_t[:]))
-                nc.vector.tensor_copy(out=pab[t][:, 1, :], in_=y[t][:].indirect(n2_t[:]))
-                d = work.tile([P, 2, S], F32, name="d", tag="d")
-                nc.vector.tensor_tensor(out=d[:], in0=pab[t][:], in1=y_ps[t][:].unsqueeze(1).to_broadcast([P, 2, S]), op=ALU.subtract)
-                dsq = keep.tile([P, 2, S], F32, name="dsq", tag="dsq")
-                nc.scalar.activation(out=dsq[:], in_=d[:], func=ACT.Square)
-                nc.scalar.activation(out=kr[t][:], in_=dsq[:], func=ACT.Exp, scale=-0.5)
-                add_turned(ksum, kr[t], e)
-                if t < 2:
-                    ms = slice(t * (P // 2), (t + 1) * (P // 2))
-                    nc.scalar.copy(out=w2_walk[:, ms], in_=w2_src[:, ms])
             for g in range(2):
-                den2[u, g] = keep.tile([P, 2, P, 2], F32, name=f"den2_{u}{g}")
-                nc.scalar.activation(out=den2[u, g][:], in_=ksum[g][:].rearrange("p c e m -> p c m e"), func=ACT.Square, bias=0.5)
+                ksum[u, g] = psum.tile([P, 2, 2, P], F32, name=f"ksum{u}{g}", tag=f"bank{PACK + 2 * u + g}")
+        dsq = {}
 
+        def weights(i):
+            t, a = divmod(i, 2)
+            nc.scalar.activation(out=kr[t][:, a, :], in_=dsq[i][:], func=ACT.Exp, scale=-0.5)
+            if a == 1:
+                for g in range(2):
+                    add_turned(ksum[t // 2, g], kr[t], t % 2, g)
+
+        steps = 2 * PACK
+        first_den_step = PACK + 1
+        for i in range(steps):
+            t, a = divmod(i, 2)
+            nc.vector.tensor_copy(out=pab[t][:, a, :], in_=y[t][:].indirect((n1_t, n2_t)[a][:]))
+            d = work.tile([P, S], F32, name="d", tag="d", bufs=4)
+            if i < steps - 1:
+                nc.gpsimd.tensor_tensor(out=d[:], in0=pab[t][:, a, :], in1=y[t][:, :S], op=ALU.subtract)
+                dsq[i] = work.tile([P, S], F32, name="dsq", tag="dsq")
+            else:
+                nc.vector.tensor_tensor(out=d[:], in0=pab[t][:, a, :], in1=y_ps_last[:], op=ALU.subtract)
+                dsq[i] = keep.tile([P, S], F32, name="dsq_last", tag="last", align_bytes=MX_ALIGN)
+            nc.scalar.activation(out=dsq[i][:], in_=d[:], func=ACT.Square)
+            if i > 0:
+                weights(i - 1)
+            if i in (first_den_step, first_den_step + 1):
+                square_den(0, i - first_den_step)
+        weights(steps - 1)
+
+        y4 = {}
+        y4[LAST] = keep.tile([P, W], F32, name="y4_3")
+        nc.vector.tensor_copy(out=y4[LAST][:], in_=y[LAST][:].indirect(n4_t[:]))
+
+        prods = keep.tile([P, PACK, 2, S], F32, name="prods", tag=f"y{LAST}")
         num = {}
         for u in range(2):
-            banks = [psum.tile([P, 2, 2, P], F32, name=f"num{u}{g}", tag=f"bank{2 * u + g}") for g in range(2)]
-            for e in range(2):
-                t = 2 * u + e
-                prod = work.tile([P, 2, S], F32, name="prod", tag="d")
-                nc.vector.scalar_tensor_tensor(out=prod[:], in0=kr[t][:], scalar=gn_t[:, t : t + 1], in1=pab[t][:], op0=ALU.mult, op1=ALU.mult)
-                add_turned(banks, prod, e)
             for g in range(2):
-                num[u, g] = banks[g]
-        nc.vector.quantize_mx(out=w2_codes[:].bitcast(FP8X4), scales=w2_scales[:], in_=w2_bf[:].rearrange("p t m j -> p (t m j)"))
-
-        rec_all = keep.tile([P, 4, 2, P, 2], F32, name="rec_all", tag="dsq")
-        rec = {}
-        for g in range(2):
-            for u in range(2):
-                rec[u, g] = rec_all[:, 2 * g + u]
-                nc.scalar.activation(out=rec[u, g], in_=den2[u, g][:], func=ACT.Abs_reciprocal_sqrt)
-
-        z_codes, z_scales = [], []
-        for g in range(2):
-            z_ps = psum.tile([P, 2, 2, P], F32, name=f"z_ps{g}", tag=f"bank{6 + g}")
-            for u in range(2):
-                zt = keep.tile([P, 2, P, 2], BF16, name=f"zt{u}{g}")
-                nc.vector.tensor_tensor(out=zt[:], in0=num[u, g][:].rearrange("p c e m -> p c m e"), in1=rec[u, g], op=ALU.mult)
-                words = zt[:].rearrange("p c m e -> p (c m e)").bitcast(F32)
-                for c in range(2):
-                    nc.tensor.transpose(z_ps[:, u, c, :], words[:, c * P : (c + 1) * P], ident[:])
-            z_bf = keep.tile([P, HALF * PACK], BF16, name=f"z_bf{g}", tag=f"z_bf{g}", align_bytes=64)
-            nc.scalar.copy(out=z_bf[:].bitcast(F32).rearrange("p (n u) -> p n u", u=2), in_=z_ps[:].rearrange("p u c n -> p (c n) u"))
-            z_codes.append(keep.tile([P, HALF], U32, name=f"z_codes{g}", align_bytes=64))
-            z_scales.append(keep.tile([P, HALF], U8, name=f"z_scales{g}", align_bytes=64))
-            nc.vector.quantize_mx(out=z_codes[g][:].bitcast(FP8X4), scales=z_scales[g][:], in_=z_bf[:])
-
-        h_ps = [psum.tile([P, S], F32, name=f"h_ps{t}", tag=f"bank{(4, 5, 0, 2)[t]}") for t in range(PACK)]
+                num[u, g] = psum.tile([P, 2, 2, P], F32, name=f"num{u}{g}", tag=f"bank{2 * u + g}")
         for g in range(2):
             cols = slice(g * HALF, (g + 1) * HALF)
             for t in range(PACK):
-                m = slice(t * P, (t + 1) * P)
-                nc.tensor.matmul_mx(out=h_ps[t][:, cols], lhsT=w2_codes[:, m].bitcast(FP8X4), lhsT_scale=w2_scales[:, m],
-                                    rhs=z_codes[g][:].bitcast(FP8X4), rhs_scale=z_scales[g][:], start=True, stop=True)
+                nc.vector.scalar_tensor_tensor(out=prods[:, t, :, cols], in0=kr[t][:, :, cols], scalar=gn_t[:, t : t + 1],
+                                               in1=pab[t][:, :, cols], op0=ALU.mult, op1=ALU.mult)
+                add_turned(num[t // 2, g], prods[:, t], t % 2, g)
+        w2_bf.append(keep.tile([P, 2, P, PACK], BF16, name="w2_bf1", tag=f"kr{LAST}", align_bytes=MX_ALIGN))
+        nc.vector.tensor_copy(out=w2_bf[1][:].rearrange("p e m j -> p m j e"), in_=w2_src[:, :, :, 2:4])
+        w2_codes = keep.tile([P, N], U32, name="w2_codes", tag=f"pab{LAST}", align_bytes=MX_ALIGN)
+        for u in range(2):
+            cols = slice(u * N // 2, (u + 1) * N // 2)
+            nc.vector.quantize_mx(out=w2_codes[:, cols].bitcast(FP8X4), scales=w2_scales[:, cols], in_=w2_bf[u][:].rearrange("p e m j -> p (e m j)"))
 
-        y4a = keep.tile([P, W], F32, name="y4a", tag="dsq")
-        y4b = keep.tile([P, W], F32, name="y4b", tag="z_bf0", align_bytes=64)
-        y4c = keep.tile([P, 2, W], F32, name="y4c", tag="z_bf1", align_bytes=64)
-        y4 = [y4a[:], y4b[:], y4c[:, 0, :], y4c[:, 1, :]]
-        for t in range(PACK):
-            nc.vector.tensor_copy(out=y4[t], in_=y[t][:].indirect(n4_t[:]))
+        rec = {}
+        rec_tags = {(0, 0): "last", (1, 0): "rec10", (0, 1): "den2_10", (1, 1): "rec11"}
+        for g in range(2):
+            for u in range(2):
+                if u == 1:
+                    square_den(1, g)
+                rec[u, g] = keep.tile([P, 2, P, 2], F32, name=f"rec{u}{g}", tag=rec_tags[u, g], align_bytes=MX_ALIGN)
+                nc.scalar.activation(out=rec[u, g][:], in_=den2[u, g][:], func=ACT.Abs_reciprocal_sqrt)
 
-        outv = out.rearrange("(p t) n -> p t n", t=PACK)
+        zt = {}
         hs = [keep.tile([P, S], F32, name=f"hs{t}") for t in range(PACK)]
+
+        def make_z(u, g, chunks):
+            nc.vector.tensor_tensor(out=zt[u, g][:, chunks], in0=num[u, g][:, chunks].rearrange("q c e p -> q c p e"),
+                                    in1=rec[u, g][:, chunks], op=ALU.mult)
+
+        def quantise_z(name, g, chunks, z_bank, codes_tag):
+            width = len(chunks) * P
+            z_ps = psum.tile([P, 2, width], F32, name=f"z_ps{name}", tag=f"bank{z_bank}")
+            for u in range(2):
+                words = zt[u, g][:].rearrange("q c p e -> q (c p e)").bitcast(F32)
+                for n, c in enumerate(chunks):
+                    nc.tensor.transpose(z_ps[:, u, n * P : (n + 1) * P], words[:, c * P : (c + 1) * P], ident[:])
+            z_bf = keep.tile([P, width * PACK], BF16, name=f"z_bf{name}", tag=f"z_bf{name}", align_bytes=MX_ALIGN)
+            nc.scalar.copy(out=z_bf[:].bitcast(F32).rearrange("p (n u) -> p n u", u=2), in_=z_ps[:].rearrange("p u n -> p n u"))
+            z_codes = keep.tile([P, width], U32, name=f"z_codes{name}", tag=codes_tag, align_bytes=MX_ALIGN)
+            z_scales = keep.tile([P, width], U8, name=f"z_scales{name}", align_bytes=MX_ALIGN)
+            nc.vector.quantize_mx(out=z_codes[:].bitcast(FP8X4), scales=z_scales[:], in_=z_bf[:])
+            return z_codes, z_scales
+
+        def second_product(h_out, t, z):
+            features = slice(t * P, (t + 1) * P)
+            nc.tensor.matmul_mx(out=h_out, lhsT=w2_codes[:, features].bitcast(FP8X4), lhsT_scale=w2_scales[:, features],
+                                rhs=z[0][:].bitcast(FP8X4), rhs_scale=z[1][:], start=True, stop=True)
+
+        for g in range(2):
+            for u in range(2):
+                zt[u, g] = keep.tile([P, 2, P, 2], BF16, name=f"zt{u}{g}")
+        make_z(0, 0, slice(0, 2))
+        make_z(1, 0, slice(0, 2))
+        make_z(0, 1, slice(0, 2))
+        make_z(1, 1, slice(0, 1))
+        make_z(1, 1, slice(1, 2))
+        z_parts = [
+            (slice(0, 2 * P), quantise_z("a", 0, (0, 1), PACK, "rec11")),
+            (slice(2 * P, 3 * P), quantise_z("b", 1, (0,), PACK + 1, "z_codes_b")),
+            (slice(3 * P, 4 * P), quantise_z("c", 1, (1,), PACK + 2, "z_codes_c")),
+        ]
+
+        h_first = psum.tile([P, 3 * P], F32, name="h_first", tag="bank4")
+        h_last = psum.tile([P, P], F32, name="h_last", tag="bank1")
+        for cols, z in z_parts[:2]:
+            second_product(h_first[:, cols], 0, z)
+        second_product(h_last[:], 0, z_parts[2][1])
+        nc.scalar.copy(out=hs[0][:, : 3 * P], in_=h_first[:])
+        nc.scalar.copy(out=hs[0][:, 3 * P :], in_=h_last[:])
+        for t, bank in ((1, "bank0"), (2, "bank2"), (3, "bank7")):
+            h_ps = psum.tile([P, S], F32, name=f"h_ps{t}", tag=bank)
+            for cols, z in z_parts:
+                second_product(h_ps[:, cols], t, z)
+            nc.scalar.copy(out=hs[t][:], in_=h_ps[:])
+
+        y4[0] = keep.tile([P, W], F32, name="y4_0", tag="z_bfa", align_bytes=MX_ALIGN)
+        y4_late = keep.tile([P, 2, W], F32, name="y4_late", tag="z_bfc", align_bytes=MX_ALIGN)
+        y4[1], y4[2] = y4_late[:, 0, :], y4_late[:, 1, :]
+        for t in range(LAST):
+            nc.vector.tensor_copy(out=y4[t][:], in_=y[t][:].indirect(n4_t[:]))
+
+        out_tiles = out.rearrange("(p t) n -> p t n", t=PACK)
         h3 = [keep.tile([P, W], F32, name=f"h3_{t}") for t in range(PACK)]
-        for t in range(PACK):
-            nc.scalar.copy(out=hs[t][:], in_=h_ps[t][:])
         for t in range(PACK):
             nc.vector.tensor_scalar(out=h3[t][:], in0=hs[t][:].indirect(n3_t[:]), scalar1=-0.5, scalar2=0.0, op0=ALU.mult, op1=ALU.add)
         for t in range(PACK):
-            nc.vector.tensor_tensor(out=hs[t][:].indirect(n3_t[:]), in0=h3[t][:], in1=y4[t], op=ALU.add)
-            nc.sync.dma_start(out=outv[:, t, :], in_=hs[t][:])
+            nc.vector.tensor_tensor(out=hs[t][:].indirect(n3_t[:]), in0=h3[t][:], in1=y4[t][:], op=ALU.add)
+            nc.sync.dma_start(out=out_tiles[:, t, :], in_=hs[t][:])

from contextlib import ExitStack

import concourse.mybir as mybir
from concourse.masks import make_identity

F32 = mybir.dt.float32
BF16 = mybir.dt.bfloat16
I32 = mybir.dt.int32
U32 = mybir.dt.uint32
U16 = mybir.dt.uint16
U8 = mybir.dt.uint8
FP8X4 = mybir.dt.float8_e4m3fn_x4
ALU = mybir.AluOpType
ACT = mybir.ActivationFunctionType

P = 128
PACK = 4
LAST = PACK - 1
QUADRANTS = 4
SCALE_ROWS = 4
STRIPE = 16
MX_ALIGN = 64
K, T, S, N, H, W = 512, 2048, 512, 512, 512, 256
HALF = S // 2
FLOPS = 2 * K * H * S + 2 * H * N * S


def tile_picked_skipputbkern_none_p_kernel(tc, x_words, x_scales, w1, gn, w2, offs, n1, n2, n3, n4, out):
    nc = tc.nc
    with ExitStack() as ctx:
        keep = ctx.enter_context(tc.tile_pool(name="keep", bufs=1))
        work = ctx.enter_context(tc.tile_pool(name="work", bufs=2))
        psum = ctx.enter_context(tc.psum_pool(name="psum", bufs=1))

        offs_t = keep.tile([P, S // STRIPE], U16, name="offs_t")
        n1_t = keep.tile([P, S // STRIPE], U16, name="n1_t")
        n2_t = keep.tile([P, S // STRIPE], U16, name="n2_t")
        n3_t = keep.tile([P, W // STRIPE], U16, name="n3_t")
        n4_t = keep.tile([P, W // STRIPE], U16, name="n4_t")
        gn_t = keep.tile([P, PACK], F32, name="gn_t")
        xw = keep.tile([P, T], I32, name="xw", align_bytes=MX_ALIGN)
        xs = keep.tile([P, T], U8, name="xs", align_bytes=MX_ALIGN)
        w1_raw = [keep.tile([P, PACK, H // 2], F32, name=f"w1_raw{h}") for h in range(2)]
        w2_raw = keep.tile([P, PACK, N], F32, name="w2_raw")
        y = [keep.tile([P, 2 * S], F32, name=f"y{t}", tag=f"y{t}") for t in range(PACK)]

        nc.gpsimd.memset(xs[:].bitcast(I32), 0)
        w1_rows = w1.rearrange("(p j) c -> p j c", j=PACK)
        nc.sync.dma_start(out=w1_raw[0][:], in_=w1_rows[:, :, : H // 2])
        nc.sync.dma_start(out=w1_raw[1][:], in_=w1_rows[:, :, H // 2 :])
        for q in range(QUADRANTS):
            rows = x_scales[0, SCALE_ROWS * q : SCALE_ROWS * (q + 1), :]
            nc.sync.dma_start(out=xs[32 * q : 32 * q + SCALE_ROWS, :].bitcast(I32), in_=rows.bitcast(I32))
        nc.sync.dma_start(out=offs_t[:], in_=offs)
        nc.sync.dma_start(out=xw[:], in_=x_words[0].rearrange("p n t -> p (n t)").bitcast(I32))
        nc.sync.dma_start(out=n1_t[:], in_=n1)
        nc.sync.dma_start(out=n2_t[:], in_=n2)
        nc.sync.dma_start(out=gn_t[:], in_=gn.rearrange("(p t) o -> p (t o)", t=PACK))
        nc.sync.dma_start(out=w2_raw[:], in_=w2.rearrange("(p j) c -> p j c", j=PACK))
        nc.sync.dma_start(out=n4_t[:], in_=n4)
        nc.sync.dma_start(out=n3_t[:], in_=n3)
        for t in range(PACK):
            nc.gpsimd.memset(y[t][:, S:], 0.0)
        ident = keep.tile([P, P], F32, name="ident")
        make_identity(nc, ident[:])

        w1_bf = keep.tile([P, PACK, P, PACK], BF16, name="w1_bf", align_bytes=MX_ALIGN)
        w1_walk = w1_bf[:].rearrange("p t m j -> p m j t")
        nc.scalar.copy(out=w1_walk[:, : P // 2], in_=w1_raw[0][:].rearrange("p j (m t) -> p m j t", t=PACK))
        nc.vector.tensor_copy(out=w1_walk[:, P // 2 :], in_=w1_raw[1][:].rearrange("p j (m t) -> p m j t", t=PACK))
        w1_codes = keep.tile([P, H], U32, name="w1_codes", align_bytes=MX_ALIGN)
        w1_scales = keep.tile([P, H], U8, name="w1_scales", align_bytes=MX_ALIGN)
        xg_scales = keep.tile([P, S], U8, name="xg_scales", align_bytes=MX_ALIGN)
        nc.vector.tensor_copy(out=xg_scales[:], in_=xs[:].indirect(offs_t[:]))
        nc.vector.quantize_mx(out=w1_codes[:].bitcast(FP8X4), scales=w1_scales[:], in_=w1_bf[:].rearrange("p t m j -> p (t m j)"))

        xg = [keep.tile([P, HALF], U32, name=f"xg{h}", tag=f"xg{h}", align_bytes=MX_ALIGN) for h in range(2)]
        for h in range(2):
            entries = offs_t[:, h * (HALF // STRIPE) : (h + 1) * (HALF // STRIPE)]
            nc.vector.tensor_copy(out=xg[h][:], in_=xw[:].bitcast(U32).indirect(entries))
        y_ps = {}
        y_ps_last = psum.tile([P, S], F32, name="y_ps_last", tag=f"bank{LAST}")
        passes = [(0, 0)] + [step for t in range(1, LAST) for step in ((t, 0), (t - 1, 1))] + [(LAST - 1, 1), (LAST, 0), (LAST, 1)]
        for t, h in passes:
            cols = slice(h * HALF, (h + 1) * HALF)
            features = slice(t * P, (t + 1) * P)
            if t < LAST:
                y_ps[t, h] = psum.tile([P, HALF], F32, name=f"y_ps{h}{t}", tag=f"bank{PACK * h + t}")[:]
            else:
                y_ps[t, h] = y_ps_last[:, cols]
            nc.tensor.matmul_mx(out=y_ps[t, h], lhsT=w1_codes[:, features].bitcast(FP8X4), lhsT_scale=w1_scales[:, features],
                                rhs=xg[h][:].bitcast(FP8X4), rhs_scale=xg_scales[:, cols], start=True, stop=True)
        vector_copy = (1, 0)
        for t in range(LAST):
            for h in range(2):
                cols = slice(h * HALF, (h + 1) * HALF)
                if (t, h) == vector_copy:
                    nc.vector.tensor_copy(out=y[t][:, cols], in_=y_ps[t, h])
                else:
                    nc.scalar.copy(out=y[t][:, cols], in_=y_ps[t, h])
        nc.scalar.copy(out=y[LAST][:, :S], in_=y_ps_last[:])

        w2_src = w2_raw[:].rearrange("p j (m t) -> p m j t", t=PACK)
        w2_bf = [keep.tile([P, 2, P, PACK], BF16, name="w2_bf0", tag="xg1", align_bytes=MX_ALIGN)]
        nc.scalar.copy(out=w2_bf[0][:].rearrange("p e m j -> p m j e"), in_=w2_src[:, :, :, 0:2])

        w2_scales = keep.tile([P, N], U8, name="w2_scales", align_bytes=MX_ALIGN)
        pab = [keep.tile([P, 2, S], F32, name=f"pab{t}", tag=f"pab{t}", align_bytes=MX_ALIGN) for t in range(PACK)]
        kr = [keep.tile([P, 2, S], F32, name=f"kr{t}", tag=f"kr{t}", align_bytes=MX_ALIGN) for t in range(PACK)]

        def add_turned(bank, src, e, g):
            for c in range(2):
                places = slice((2 * g + c) * P, (2 * g + c + 1) * P)
                for a in range(2):
                    nc.tensor.matmul(bank[:, c, e, :], lhsT=src[:, a, places], rhs=ident[:], start=(a == 0), stop=(a == 1), is_transpose=True)

        ksum, den2 = {}, {}

        def square_den(u, g):
            den2[u, g] = keep.tile([P, 2, P, 2], F32, name=f"den2_{u}{g}", tag=f"den2_{u}{g}", align_bytes=MX_ALIGN)
            nc.scalar.activation(out=den2[u, g][:], in_=ksum[u, g][:].rearrange("q c e p -> q c p e"), func=ACT.Square, bias=0.5)

        for u in range(2):
            for g in range(2):
                ksum[u, g] = psum.tile([P, 2, 2, P], F32, name=f"ksum{u}{g}", tag=f"bank{PACK + 2 * u + g}")
        dsq = {}

        def weights(i):
            t, a = divmod(i, 2)
            nc.scalar.activation(out=kr[t][:, a, :], in_=dsq[i][:], func=ACT.Exp, scale=-0.5)
            if a == 1:
                for g in range(2):
                    add_turned(ksum[t // 2, g], kr[t], t % 2, g)

        steps = 2 * PACK
        first_den_step = PACK + 1
        for i in range(steps):
            t, a = divmod(i, 2)
            nc.vector.tensor_copy(out=pab[t][:, a, :], in_=y[t][:].indirect((n1_t, n2_t)[a][:]))
            d = work.tile([P, S], F32, name="d", tag="d", bufs=4)
            if i < steps - 1:
                nc.gpsimd.tensor_tensor(out=d[:], in0=pab[t][:, a, :], in1=y[t][:, :S], op=ALU.subtract)
                dsq[i] = work.tile([P, S], F32, name="dsq", tag="dsq")
            else:
                nc.vector.tensor_tensor(out=d[:], in0=pab[t][:, a, :], in1=y_ps_last[:], op=ALU.subtract)
                dsq[i] = keep.tile([P, S], F32, name="dsq_last", tag="last", align_bytes=MX_ALIGN)
            nc.scalar.activation(out=dsq[i][:], in_=d[:], func=ACT.Square)
            if i > 0:
                weights(i - 1)
            if i in (first_den_step, first_den_step + 1):
                square_den(0, i - first_den_step)
        weights(steps - 1)

        y4 = {}
        y4[LAST] = keep.tile([P, W], F32, name="y4_3")
        nc.vector.tensor_copy(out=y4[LAST][:], in_=y[LAST][:].indirect(n4_t[:]))

        prods = keep.tile([P, PACK, 2, S], F32, name="prods", tag=f"y{LAST}")
        num = {}
        for u in range(2):
            for g in range(2):
                num[u, g] = psum.tile([P, 2, 2, P], F32, name=f"num{u}{g}", tag=f"bank{2 * u + g}")
        for g in range(2):
            cols = slice(g * HALF, (g + 1) * HALF)
            for t in range(PACK):
                nc.vector.scalar_tensor_tensor(out=prods[:, t, :, cols], in0=kr[t][:, :, cols], scalar=gn_t[:, t : t + 1],
                                               in1=pab[t][:, :, cols], op0=ALU.mult, op1=ALU.mult)
                add_turned(num[t // 2, g], prods[:, t], t % 2, g)
        w2_bf.append(keep.tile([P, 2, P, PACK], BF16, name="w2_bf1", tag=f"kr{LAST}", align_bytes=MX_ALIGN))
        nc.vector.tensor_copy(out=w2_bf[1][:].rearrange("p e m j -> p m j e"), in_=w2_src[:, :, :, 2:4])
        w2_codes = keep.tile([P, N], U32, name="w2_codes", tag=f"pab{LAST}", align_bytes=MX_ALIGN)
        for u in range(2):
            cols = slice(u * N // 2, (u + 1) * N // 2)
            nc.vector.quantize_mx(out=w2_codes[:, cols].bitcast(FP8X4), scales=w2_scales[:, cols], in_=w2_bf[u][:].rearrange("p e m j -> p (e m j)"))

        rec = {}
        rec_tags = {(0, 0): "last", (1, 0): "rec10", (0, 1): "den2_10", (1, 1): "rec11"}
        for g in range(2):
            for u in range(2):
                if u == 1:
                    square_den(1, g)
                rec[u, g] = keep.tile([P, 2, P, 2], F32, name=f"rec{u}{g}", tag=rec_tags[u, g], align_bytes=MX_ALIGN)
                nc.scalar.activation(out=rec[u, g][:], in_=den2[u, g][:], func=ACT.Abs_reciprocal_sqrt)

        zt = {}
        hs = [keep.tile([P, S], F32, name=f"hs{t}") for t in range(PACK)]

        def make_z(u, g, chunks):
            nc.vector.tensor_tensor(out=zt[u, g][:, chunks], in0=num[u, g][:, chunks].rearrange("q c e p -> q c p e"),
                                    in1=rec[u, g][:, chunks], op=ALU.mult)

        def quantise_z(name, g, chunks, z_bank, codes_tag):
            width = len(chunks) * P
            z_ps = psum.tile([P, 2, width], F32, name=f"z_ps{name}", tag=f"bank{z_bank}")
            for u in range(2):
                words = zt[u, g][:].rearrange("q c p e -> q (c p e)").bitcast(F32)
                for n, c in enumerate(chunks):
                    nc.tensor.transpose(z_ps[:, u, n * P : (n + 1) * P], words[:, c * P : (c + 1) * P], ident[:])
            z_bf = keep.tile([P, width * PACK], BF16, name=f"z_bf{name}", tag=f"z_bf{name}", align_bytes=MX_ALIGN)
            nc.scalar.copy(out=z_bf[:].bitcast(F32).rearrange("p (n u) -> p n u", u=2), in_=z_ps[:].rearrange("p u n -> p n u"))
            z_codes = keep.tile([P, width], U32, name=f"z_codes{name}", tag=codes_tag, align_bytes=MX_ALIGN)
            z_scales = keep.tile([P, width], U8, name=f"z_scales{name}", align_bytes=MX_ALIGN)
            nc.vector.quantize_mx(out=z_codes[:].bitcast(FP8X4), scales=z_scales[:], in_=z_bf[:])
            return z_codes, z_scales

        def second_product(h_out, t, z):
            features = slice(t * P, (t + 1) * P)
            nc.tensor.matmul_mx(out=h_out, lhsT=w2_codes[:, features].bitcast(FP8X4), lhsT_scale=w2_scales[:, features],
                                rhs=z[0][:].bitcast(FP8X4), rhs_scale=z[1][:], start=True, stop=True)

        for g in range(2):
            for u in range(2):
                zt[u, g] = keep.tile([P, 2, P, 2], BF16, name=f"zt{u}{g}")
        make_z(0, 0, slice(0, 2))
        make_z(1, 0, slice(0, 2))
        make_z(0, 1, slice(0, 2))
        make_z(1, 1, slice(0, 1))
        make_z(1, 1, slice(1, 2))
        z_parts = [
            (slice(0, 2 * P), quantise_z("a", 0, (0, 1), PACK, "rec11")),
            (slice(2 * P, 3 * P), quantise_z("b", 1, (0,), PACK + 1, "z_codes_b")),
            (slice(3 * P, 4 * P), quantise_z("c", 1, (1,), PACK + 2, "z_codes_c")),
        ]

        h_first = psum.tile([P, 3 * P], F32, name="h_first", tag="bank4")
        h_last = psum.tile([P, P], F32, name="h_last", tag="bank1")
        for cols, z in z_parts[:2]:
            second_product(h_first[:, cols], 0, z)
        second_product(h_last[:], 0, z_parts[2][1])
        nc.scalar.copy(out=hs[0][:, : 3 * P], in_=h_first[:])
        nc.scalar.copy(out=hs[0][:, 3 * P :], in_=h_last[:])
        for t, bank in ((1, "bank0"), (2, "bank2"), (3, "bank7")):
            h_ps = psum.tile([P, S], F32, name=f"h_ps{t}", tag=bank)
            for cols, z in z_parts:
                second_product(h_ps[:, cols], t, z)
            nc.scalar.copy(out=hs[t][:], in_=h_ps[:])

        y4[0] = keep.tile([P, W], F32, name="y4_0", tag="z_bfa", align_bytes=MX_ALIGN)
        y4_late = keep.tile([P, 2, W], F32, name="y4_late", tag="z_bfc", align_bytes=MX_ALIGN)
        y4[1], y4[2] = y4_late[:, 0, :], y4_late[:, 1, :]
        for t in range(LAST):
            nc.vector.tensor_copy(out=y4[t][:], in_=y[t][:].indirect(n4_t[:]))

        out_tiles = out.rearrange("(p t) n -> p t n", t=PACK)
        h3 = [keep.tile([P, W], F32, name=f"h3_{t}") for t in range(PACK)]
        for t in range(PACK):
            nc.vector.tensor_scalar(out=h3[t][:], in0=hs[t][:].indirect(n3_t[:]), scalar1=-0.5, scalar2=0.0, op0=ALU.mult, op1=ALU.add)
        for t in range(PACK):
            nc.vector.tensor_tensor(out=hs[t][:].indirect(n3_t[:]), in0=h3[t][:], in1=y4[t][:], op=ALU.add)
            nc.sync.dma_start(out=out_tiles[:, t, :], in_=hs[t][:])
